import numpy as np, ml_dtypes
CORES = [24,48,72,152,176,200]
N = 6
TK = 32
def setup_inputs(rng):
    return {"c": rng.standard_normal((N, 128, 128), dtype=np.float32).astype(ml_dtypes.bfloat16), "x": rng.standard_normal((N, 128, TK), dtype=np.float32).astype(ml_dtypes.bfloat16)}
def setup_inputs_big(rng):
    d = setup_inputs(rng)
    for k in ("c", "x"): d[k] = (d[k].astype(np.float32) * 1024.0).astype(d[k].dtype)
    return d
def setup_inputs_small(rng):
    d = setup_inputs(rng)
    for k in ("c", "x"): d[k] = (d[k].astype(np.float32) * (1 / 1024.0)).astype(d[k].dtype)
    return d
def setup_inputs_apart(rng):
    d = setup_inputs(rng)
    f = (10.0 ** rng.permutation(np.linspace(-1.5, 1.5, N))).astype(np.float32).reshape(N, 1, 1)
    for k in ("c", "x"): d[k] = (d[k].astype(np.float32) * f).astype(d[k].dtype)
    return d
def reference(c, x):
    C, X = c.astype(np.float64), x.astype(np.float64)
    y = np.zeros((N, 128, TK))
    for r in range(N):
        for j in range(N):
            y[r] += C[(r - j) % N].T @ X[j]
    return {"y": y.astype(ml_dtypes.bfloat16 if x.dtype != np.float64 else np.float64)}

@@ -1,0 +1,123 @@
+from concourse.bass import DstId, RemoteDMATransfer
+
+WORLD = 256
+KC, TK = 128, 32
+W = KC + TK
+
+SCRATCH = {
+    "blk": ("sbuf", [128, 6 * W], "bfloat16"),
+    "acc": ("psum", [128, TK], "float32"),
+    "yb": ("sbuf", [128, TK], "bfloat16"),
+}
+SEMAPHORES = ["ld", "got", "dirs", "rel", "sent", "mm", "cp", "st"]
+
+
+def _bits(mask):
+    return [b for b in range(mask.bit_length()) if (mask >> b) & 1]
+
+
+def _mask(bits):
+    m = 0
+    for b in bits:
+        m |= 1 << b
+    return m
+
+
+def _plan(T, topo):
+    cores = list(T.cores)
+    n = len(cores)
+    plan = []
+    turn = {}
+    for s, sc in enumerate(cores):
+        near = [d for d in range(n) if d != s and topo.may_write(sc, cores[d])]
+        far = [d for d in range(n) if d != s and not topo.may_write(sc, cores[d])]
+        owners = [h for h in range(WORLD)
+                  if h != sc and topo.host(h) == topo.host(sc) and topo.chip(h) == topo.chip(sc)
+                  and all(topo.may_write(h, cores[d]) for d in far)]
+        relays = []
+        for h in owners:
+            if topo.die(h) not in [topo.die(q) for q in relays]:
+                relays.append(h)
+        t = turn.get(tuple(far), 0)
+        turn[tuple(far)] = t + 1
+        share = [[] for _ in relays]
+        for i, d in enumerate(far):
+            share[(i + t) % len(relays)].append(d)
+        plan.append((near, [(h, sh) for h, sh in zip(relays, share) if sh]))
+    return plan
+
+
+def _send(g, topo, T, core, slot, dsts, mask, remote_sem):
+    ids = []
+    for d in dsts:
+        rid, pid = topo.addr(d, core)
+        ids.append(DstId(rid=rid, pnc=pid))
+    g.remote_dma_fused([RemoteDMATransfer(dst_ids=ids, dma_engine_mask=mask, remote_sem=remote_sem,
+                                          srcs=[slot], dsts=[slot for _ in dsts], alu_op=0)],
+                       local_sem=T.sem.sent)
+
+
+def rank_program(g, core, T, topo):
+    cores = list(T.cores)
+    n = len(cores)
+    plan = _plan(T, topo)
+    rank = T.rank_of(core)
+
+    def slot(s):
+        return T.blk[:, s * W:(s + 1) * W]
+
+    if rank is None:
+        for s in range(n):
+            for h, share in plan[s][1]:
+                if h == core:
+                    on = _bits(topo.mask(cores[s], core))
+                    off = _bits(topo.mask(cores[s], cores[plan[s][0][0]]))
+                    n_on = len([b for b in on if b not in off])
+                    out = topo.mask(core, cores[share[0]])
+                    g.wait_ge(T.sem.got, n_on)
+                    _send(g, topo, T, core, slot(s), [cores[d] for d in share], out, T.sem.rel)
+                    g.wait_ge(T.sem.sent, len(_bits(out)))
+        return
+
+    near, relays = plan[rank]
+    g.sync.dma_start(T.blk[:, rank * W:rank * W + KC], T.c[:, :]).then_inc(T.sem.ld, 16)
+    g.scalar.dma_start(T.blk[:, rank * W + KC:(rank + 1) * W], T.x[:, :]).then_inc(T.sem.ld, 16)
+    g.wait_ge(T.sem.ld, 32)
+
+    off = _bits(topo.mask(core, cores[near[0]]))
+    on = [b for b in _bits(topo.mask(core, relays[0][0])) if b not in off]
+    _send(g, topo, T, core, slot(rank), [h for h, _ in relays], _mask(on), T.sem.got)
+    _send(g, topo, T, core, slot(rank), [cores[d] for d in near], _mask(off), T.sem.dirs)
+
+    n_dir = 0
+    for s in near:
+        n_dir += len(_bits(topo.mask(cores[s], core)))
+    n_rel = 0
+    for s in range(n):
+        for h, share in plan[s][1]:
+            if rank in share:
+                n_rel += len(_bits(topo.mask(h, core)))
+
+    have = [rank] + near
+    pairs = [(k, (rank - k) % n) for k in range(n)]
+    early = [p for p in pairs if p[0] in have and p[1] in have]
+    late = [p for p in pairs if p not in early]
+    te = g.tensor
+    te.wait_ge(T.sem.ld, 32)
+    te.wait_ge(T.sem.dirs, n_dir)
+    done = 0
+    for group in (early, late):
+        if group is late:
+            te.wait_ge(T.sem.rel, n_rel)
+        for k, j in group:
+            mm = te.matmul(T.acc[:, :], T.blk[:, k * W:k * W + KC], T.blk[:, j * W + KC:(j + 1) * W],
+                           done == 0, done == n - 1)
+            done += 1
+            if done == n:
+                mm.then_inc(T.sem.mm, 1)
+    g.vector.wait_ge(T.sem.mm, 1)
+    g.vector.tensor_copy(T.yb[:, :], T.acc[:, :]).then_inc(T.sem.cp, 1)
+    g.sync.wait_ge(T.sem.cp, 1)
+    g.sync.dma_start(T.y[:, :], T.yb[:, :]).then_inc(T.sem.st, 16)
+    g.wait_ge(T.sem.sent, len(on) + len(off))
+    g.wait_ge(T.sem.st, 16)

@@ -5,11 +5,12 @@ KC, TK = 128, 32
 W = KC + TK
 
 SCRATCH = {
+    "pk": ("dram", [128, W], "bfloat16"),
     "blk": ("sbuf", [128, 6 * W], "bfloat16"),
     "acc": ("psum", [128, TK], "float32"),
     "yb": ("sbuf", [128, TK], "bfloat16"),
 }
-SEMAPHORES = ["ld", "got", "dirs", "rel", "sent", "mm", "cp", "st"]
+SEMAPHORES = ["ld", "own", "got", "dirs", "rel0", "rel1", "rel2", "rel3", "sent", "mm", "cp", "st"]
 
 
 def _bits(mask):
@@ -34,27 +35,34 @@ def _plan(T, topo):
         owners = [h for h in range(WORLD)
                   if h != sc and topo.host(h) == topo.host(sc) and topo.chip(h) == topo.chip(sc)
                   and all(topo.may_write(h, cores[d]) for d in far)]
+        mine = [h for h in owners if topo.die(h) == topo.die(sc)]
+        other = [h for h in owners if topo.die(h) != topo.die(sc)]
         relays = []
-        for h in owners:
-            if topo.die(h) not in [topo.die(q) for q in relays]:
-                relays.append(h)
+        for a, b in zip(mine, other):
+            relays += [a, b]
         t = turn.get(tuple(far), 0)
         turn[tuple(far)] = t + 1
-        share = [[] for _ in relays]
-        for i, d in enumerate(far):
-            share[(i + t) % len(relays)].append(d)
-        plan.append((near, [(h, sh) for h, sh in zip(relays, share) if sh]))
+        served = far[::-1] if t % 2 else far
+        plan.append((near, list(zip(relays, served)), t))
     return plan
 
 
-def _send(g, topo, T, core, slot, dsts, mask, remote_sem):
+def _far_sources(plan, d):
+    out = []
+    for s in range(len(plan)):
+        for i, (h, dst) in enumerate(plan[s][1]):
+            if dst == d:
+                out.append((i // 2, s, h))
+    return sorted(out)
+
+
+def _transfer(topo, core, src, dsts, mask, remote_sem):
     ids = []
-    for d in dsts:
+    for d, _ in dsts:
         rid, pid = topo.addr(d, core)
         ids.append(DstId(rid=rid, pnc=pid))
-    g.remote_dma_fused([RemoteDMATransfer(dst_ids=ids, dma_engine_mask=mask, remote_sem=remote_sem,
-                                          srcs=[slot], dsts=[slot for _ in dsts], alu_op=0)],
-                       local_sem=T.sem.sent)
+    return RemoteDMATransfer(dst_ids=ids, dma_engine_mask=mask, remote_sem=remote_sem,
+                             srcs=[src], dsts=[ap for _, ap in dsts], alu_op=0)
 
 
 def rank_program(g, core, T, topo):
@@ -66,50 +74,53 @@ def rank_program(g, core, T, topo):
     def slot(s):
         return T.blk[:, s * W:(s + 1) * W]
 
+    def split(sc):
+        near, relays, _ = plan[T.rank_of(sc)]
+        off = _bits(topo.mask(sc, cores[near[0]]))
+        return off, [b for b in _bits(topo.mask(sc, relays[0][0])) if b not in off]
+
     if rank is None:
         for s in range(n):
-            for h, share in plan[s][1]:
+            for h, d in plan[s][1]:
                 if h == core:
-                    on = _bits(topo.mask(cores[s], core))
-                    off = _bits(topo.mask(cores[s], cores[plan[s][0][0]]))
-                    n_on = len([b for b in on if b not in off])
-                    out = topo.mask(core, cores[share[0]])
-                    g.wait_ge(T.sem.got, n_on)
-                    _send(g, topo, T, core, slot(s), [cores[d] for d in share], out, T.sem.rel)
+                    out = topo.mask(core, cores[d])
+                    g.wait_ge(T.sem.got, len(split(cores[s])[1]) // 2)
+                    g.remote_dma_fused([_transfer(topo, core, T.pk[:, :], [(cores[d], slot(s))], out,
+                                                  T.sem["rel%d" % plan[s][2]])], local_sem=T.sem.sent)
                     g.wait_ge(T.sem.sent, len(_bits(out)))
         return
 
-    near, relays = plan[rank]
-    g.sync.dma_start(T.blk[:, rank * W:rank * W + KC], T.c[:, :]).then_inc(T.sem.ld, 16)
-    g.scalar.dma_start(T.blk[:, rank * W + KC:(rank + 1) * W], T.x[:, :]).then_inc(T.sem.ld, 16)
+    near, relays, _ = plan[rank]
+    g.sync.dma_start(T.pk[:, 0:KC], T.c[:, :]).then_inc(T.sem.ld, 16)
+    g.scalar.dma_start(T.pk[:, KC:W], T.x[:, :]).then_inc(T.sem.ld, 16)
     g.wait_ge(T.sem.ld, 32)
-
-    off = _bits(topo.mask(core, cores[near[0]]))
-    on = [b for b in _bits(topo.mask(core, relays[0][0])) if b not in off]
-    _send(g, topo, T, core, slot(rank), [h for h, _ in relays], _mask(on), T.sem.got)
-    _send(g, topo, T, core, slot(rank), [cores[d] for d in near], _mask(off), T.sem.dirs)
+    off, on = split(core)
+    g.remote_dma_fused(
+        [_transfer(topo, core, T.pk[:, :], [(h, T.pk[:, :]) for h, _ in relays[1::2]], _mask(on[0::2]), T.sem.got),
+         _transfer(topo, core, T.pk[:, :], [(h, T.pk[:, :]) for h, _ in relays[0::2]], _mask(on[1::2]), T.sem.got)],
+        local_sem=T.sem.sent)
+    g.remote_dma_fused([_transfer(topo, core, T.pk[:, :], [(cores[d], slot(rank)) for d in near], _mask(off),
+                                  T.sem.dirs)], local_sem=T.sem.sent)
+    g.scalar.wait_ge(T.sem.ld, 32)
+    g.scalar.dma_start(slot(rank), T.pk[:, :]).then_inc(T.sem.own, 16)
 
     n_dir = 0
     for s in near:
         n_dir += len(_bits(topo.mask(cores[s], core)))
-    n_rel = 0
-    for s in range(n):
-        for h, share in plan[s][1]:
-            if rank in share:
-                n_rel += len(_bits(topo.mask(h, core)))
 
-    have = [rank] + near
-    pairs = [(k, (rank - k) % n) for k in range(n)]
-    early = [p for p in pairs if p[0] in have and p[1] in have]
-    late = [p for p in pairs if p not in early]
     te = g.tensor
-    te.wait_ge(T.sem.ld, 32)
+    te.wait_ge(T.sem.own, 16)
     te.wait_ge(T.sem.dirs, n_dir)
+    have = [rank] + near
+    todo = [(k, (rank - k) % n) for k in range(n)]
     done = 0
-    for group in (early, late):
-        if group is late:
-            te.wait_ge(T.sem.rel, n_rel)
-        for k, j in group:
+    for step in [None] + _far_sources(plan, rank):
+        if step is not None:
+            _, s, h = step
+            te.wait_ge(T.sem["rel%d" % plan[s][2]], len(_bits(topo.mask(h, core))))
+            have.append(s)
+        for k, j in [p for p in todo if p[0] in have and p[1] in have]:
+            todo.remove((k, j))
             mm = te.matmul(T.acc[:, :], T.blk[:, k * W:k * W + KC], T.blk[:, j * W + KC:(j + 1) * W],
                            done == 0, done == n - 1)
             done += 1

@@ -2,15 +2,18 @@ from concourse.bass import DstId, RemoteDMATransfer
 
 WORLD = 256
 KC, TK = 128, 32
-W = KC + TK
 
 SCRATCH = {
-    "pk": ("dram", [128, W], "bfloat16"),
-    "blk": ("sbuf", [128, 6 * W], "bfloat16"),
+    "pc": ("dram", [128, KC], "bfloat16"),
+    "px": ("dram", [128, TK], "bfloat16"),
+    "bc": ("sbuf", [128, 6 * KC], "bfloat16"),
+    "bx": ("sbuf", [128, 6 * TK], "bfloat16"),
     "acc": ("psum", [128, TK], "float32"),
     "yb": ("sbuf", [128, TK], "bfloat16"),
 }
-SEMAPHORES = ["ld", "own", "got", "dirs", "rel0", "rel1", "rel2", "rel3", "sent", "mm", "cp", "st"]
+SEMAPHORES = ["ldx", "ldc", "go", "own", "hx", "hc", "xs", "c0", "c1", "c2", "c3", "c4", "c5", "sent", "mm", "cp", "st"]
+
+_CACHE = {}
 
 
 def _bits(mask):
@@ -25,35 +28,59 @@ def _mask(bits):
 
 
 def _plan(T, topo):
+    if "plan" in _CACHE:
+        return _CACHE["plan"]
     cores = list(T.cores)
     n = len(cores)
+    near = [[d for d in range(n) if d != s and topo.may_write(cores[s], cores[d])] for s in range(n)]
+    direct = []
+    for s in range(n):
+        later = [d for d in near[s] if d > s]
+        direct.append(later[0] if later else near[s][0])
+    inb = {}
+    for s in range(n):
+        key = (direct[s], topo.die(cores[s]))
+        inb[key] = inb.get(key, 0) + 1
     plan = []
-    turn = {}
     for s, sc in enumerate(cores):
-        near = [d for d in range(n) if d != s and topo.may_write(sc, cores[d])]
-        far = [d for d in range(n) if d != s and not topo.may_write(sc, cores[d])]
-        owners = [h for h in range(WORLD)
-                  if h != sc and topo.host(h) == topo.host(sc) and topo.chip(h) == topo.chip(sc)
-                  and all(topo.may_write(h, cores[d]) for d in far)]
-        mine = [h for h in owners if topo.die(h) == topo.die(sc)]
-        other = [h for h in owners if topo.die(h) != topo.die(sc)]
-        relays = []
-        for a, b in zip(mine, other):
-            relays += [a, b]
-        t = turn.get(tuple(far), 0)
-        turn[tuple(far)] = t + 1
-        served = far[::-1] if t % 2 else far
-        plan.append((near, list(zip(relays, served)), t))
+        rest = [d for d in range(n) if d != s and d != direct[s]]
+        far = [d for d in rest if d not in near[s]]
+        chipmates = [h for h in range(WORLD)
+                     if h != sc and topo.host(h) == topo.host(sc) and topo.chip(h) == topo.chip(sc)]
+        owners = [h for h in chipmates if all(topo.may_write(h, cores[d]) for d in far)]
+        pools = ([h for h in chipmates if topo.die(h) == topo.die(sc)],
+                 [h for h in chipmates if topo.die(h) != topo.die(sc)])
+        best = None
+        for pick in range(1 << len(rest)):
+            groups = ([d for i, d in enumerate(rest) if (pick >> i) & 1],
+                      [d for i, d in enumerate(rest) if not (pick >> i) & 1])
+            if len(groups[0]) != len(groups[1]):
+                continue
+            cost, fits = 0, True
+            for grp, pool in zip(groups, pools):
+                nfar = len([d for d in grp if d in far])
+                if nfar > len([h for h in pool if h in owners]) or len(grp) > len(pool):
+                    fits = False
+                    break
+                cost += nfar * nfar
+                for d in grp:
+                    cost += 2 * inb.get((d, topo.die(pool[0])), 0) + 1
+            if fits and (best is None or cost < best[0]):
+                best = (cost, groups)
+        helpers = []
+        for grp, pool in zip(best[1], pools):
+            own = [h for h in pool if h in owners]
+            plain = [h for h in pool if h not in owners]
+            for d in [d for d in grp if d in far]:
+                helpers.append((own.pop(0), d))
+            for d in [d for d in grp if d not in far]:
+                helpers.append(((plain or own).pop(0), d))
+        for h, d in helpers:
+            key = (d, topo.die(h))
+            inb[key] = inb.get(key, 0) + 1
+        plan.append((direct[s], helpers))
+    _CACHE["plan"] = plan
     return plan
-
-
-def _far_sources(plan, d):
-    out = []
-    for s in range(len(plan)):
-        for i, (h, dst) in enumerate(plan[s][1]):
-            if dst == d:
-                out.append((i // 2, s, h))
-    return sorted(out)
 
 
 def _transfer(topo, core, src, dsts, mask, remote_sem):
@@ -71,64 +98,80 @@ def rank_program(g, core, T, topo):
     plan = _plan(T, topo)
     rank = T.rank_of(core)
 
-    def slot(s):
-        return T.blk[:, s * W:(s + 1) * W]
+    def cslot(s):
+        return T.bc[:, s * KC:(s + 1) * KC]
 
-    def split(sc):
-        near, relays, _ = plan[T.rank_of(sc)]
-        off = _bits(topo.mask(sc, cores[near[0]]))
-        return off, [b for b in _bits(topo.mask(sc, relays[0][0])) if b not in off]
+    def xslot(s):
+        return T.bx[:, s * TK:(s + 1) * TK]
+
+    def split(s):
+        off = _bits(topo.mask(cores[s], cores[plan[s][0]]))
+        return off, [b for b in _bits(topo.mask(cores[s], plan[s][1][0][0])) if b not in off]
 
     if rank is None:
         for s in range(n):
             for h, d in plan[s][1]:
                 if h == core:
                     out = topo.mask(core, cores[d])
-                    g.wait_ge(T.sem.got, len(split(cores[s])[1]) // 2)
-                    g.remote_dma_fused([_transfer(topo, core, T.pk[:, :], [(cores[d], slot(s))], out,
-                                                  T.sem["rel%d" % plan[s][2]])], local_sem=T.sem.sent)
-                    g.wait_ge(T.sem.sent, len(_bits(out)))
+                    part = len(split(s)[1]) // 2
+                    g.wait_ge(T.sem.hx, part)
+                    g.remote_dma_fused([_transfer(topo, core, T.px[:, :], [(cores[d], xslot(s))], out, T.sem.xs)],
+                                       local_sem=T.sem.sent)
+                    g.wait_ge(T.sem.hc, part)
+                    g.remote_dma_fused([_transfer(topo, core, T.pc[:, :], [(cores[d], cslot(s))], out,
+                                                  T.sem["c%d" % s])], local_sem=T.sem.sent)
+                    g.wait_ge(T.sem.sent, 2 * len(_bits(out)))
         return
 
-    near, relays, _ = plan[rank]
-    g.sync.dma_start(T.pk[:, 0:KC], T.c[:, :]).then_inc(T.sem.ld, 16)
-    g.scalar.dma_start(T.pk[:, KC:W], T.x[:, :]).then_inc(T.sem.ld, 16)
-    g.wait_ge(T.sem.ld, 32)
-    off, on = split(core)
-    g.remote_dma_fused(
-        [_transfer(topo, core, T.pk[:, :], [(h, T.pk[:, :]) for h, _ in relays[1::2]], _mask(on[0::2]), T.sem.got),
-         _transfer(topo, core, T.pk[:, :], [(h, T.pk[:, :]) for h, _ in relays[0::2]], _mask(on[1::2]), T.sem.got)],
-        local_sem=T.sem.sent)
-    g.remote_dma_fused([_transfer(topo, core, T.pk[:, :], [(cores[d], slot(rank)) for d in near], _mask(off),
-                                  T.sem.dirs)], local_sem=T.sem.sent)
-    g.scalar.wait_ge(T.sem.ld, 32)
-    g.scalar.dma_start(slot(rank), T.pk[:, :]).then_inc(T.sem.own, 16)
+    nxt, helpers = plan[rank]
+    g.sync.dma_start(T.px[:, :], T.x[:, :]).then_inc(T.sem.ldx, 16)
+    g.scalar.dma_start(T.pc[:, :], T.c[:, :]).then_inc(T.sem.ldc, 16)
+    off, on = split(rank)
+    mine = [h for h, _ in helpers if topo.die(h) == topo.die(core)]
+    other = [h for h, _ in helpers if topo.die(h) != topo.die(core)]
+    g.wait_ge(T.sem.ldx, 16)
+    g.remote_dma_fused([_transfer(topo, core, T.px[:, :], [(h, T.px[:, :]) for h in other], _mask(on[0::2]), T.sem.hx),
+                        _transfer(topo, core, T.px[:, :], [(h, T.px[:, :]) for h in mine], _mask(on[1::2]), T.sem.hx)],
+                       local_sem=T.sem.sent)
+    g.wait_ge(T.sem.ldc, 16)
+    g.remote_dma_fused([_transfer(topo, core, T.pc[:, :], [(h, T.pc[:, :]) for h in other], _mask(on[0::2]), T.sem.hc),
+                        _transfer(topo, core, T.pc[:, :], [(h, T.pc[:, :]) for h in mine], _mask(on[1::2]), T.sem.hc)],
+                       local_sem=T.sem.sent)
+    g.remote_dma_fused([_transfer(topo, core, T.px[:, :], [(cores[nxt], xslot(rank))], _mask(off), T.sem.xs)],
+                       local_sem=T.sem.sent)
+    g.remote_dma_fused([_transfer(topo, core, T.pc[:, :], [(cores[nxt], cslot(rank))], _mask(off),
+                                  T.sem["c%d" % rank])], local_sem=T.sem.sent)
+    g.sem_inc(T.sem.go, 1)
+    g.sync.wait_ge(T.sem.go, 1)
+    g.sync.dma_start(xslot(rank), T.x[:, :]).then_inc(T.sem.own, 16)
+    g.scalar.wait_ge(T.sem.go, 1)
+    g.scalar.dma_start(cslot(rank), T.c[:, :]).then_inc(T.sem.own, 16)
 
-    n_dir = 0
-    for s in near:
-        n_dir += len(_bits(topo.mask(cores[s], core)))
+    senders = []
+    for s in range(n):
+        if s == rank:
+            continue
+        if plan[s][0] == rank:
+            senders.append((0, s, cores[s]))
+        for h, d in plan[s][1]:
+            if d == rank:
+                senders.append((1 if topo.same_plane(h, core) else 2, s, h))
+    senders.sort()
 
     te = g.tensor
-    te.wait_ge(T.sem.own, 16)
-    te.wait_ge(T.sem.dirs, n_dir)
-    have = [rank] + near
-    todo = [(k, (rank - k) % n) for k in range(n)]
-    done = 0
-    for step in [None] + _far_sources(plan, rank):
-        if step is not None:
-            _, s, h = step
-            te.wait_ge(T.sem["rel%d" % plan[s][2]], len(_bits(topo.mask(h, core))))
-            have.append(s)
-        for k, j in [p for p in todo if p[0] in have and p[1] in have]:
-            todo.remove((k, j))
-            mm = te.matmul(T.acc[:, :], T.blk[:, k * W:k * W + KC], T.blk[:, j * W + KC:(j + 1) * W],
-                           done == 0, done == n - 1)
-            done += 1
-            if done == n:
-                mm.then_inc(T.sem.mm, 1)
+    te.wait_ge(T.sem.own, 32)
+    n_x = 0
+    for _, _, h in senders:
+        n_x += len(_bits(topo.mask(h, core)))
+    te.wait_ge(T.sem.xs, n_x)
+    mm = te.matmul(T.acc[:, :], cslot(rank), xslot(0), True, False)
+    for i, (_, s, h) in enumerate(senders):
+        te.wait_ge(T.sem["c%d" % s], len(_bits(topo.mask(h, core))))
+        mm = te.matmul(T.acc[:, :], cslot(s), xslot((rank - s) % n), False, i == len(senders) - 1)
+    mm.then_inc(T.sem.mm, 1)
     g.vector.wait_ge(T.sem.mm, 1)
     g.vector.tensor_copy(T.yb[:, :], T.acc[:, :]).then_inc(T.sem.cp, 1)
     g.sync.wait_ge(T.sem.cp, 1)
     g.sync.dma_start(T.y[:, :], T.yb[:, :]).then_inc(T.sem.st, 16)
-    g.wait_ge(T.sem.sent, len(on) + len(off))
+    g.wait_ge(T.sem.sent, 2 * len(on) + 2 * len(off))
     g.wait_ge(T.sem.st, 16)

from concourse.bass import DstId, RemoteDMATransfer

WORLD = 256
KC, TK = 128, 32

SCRATCH = {
    "pc": ("dram", [128, KC], "bfloat16"),
    "px": ("dram", [128, TK], "bfloat16"),
    "bc": ("sbuf", [128, 6 * KC], "bfloat16"),
    "bx": ("sbuf", [128, 6 * TK], "bfloat16"),
    "acc": ("psum", [128, TK], "float32"),
    "yb": ("sbuf", [128, TK], "bfloat16"),
}
SEMAPHORES = ["ldx", "ldc", "go", "own", "hx", "hc", "xs", "c0", "c1", "c2", "c3", "c4", "c5", "sent", "mm", "cp", "st"]

_CACHE = {}


def _bits(mask):
    return [b for b in range(mask.bit_length()) if (mask >> b) & 1]


def _mask(bits):
    m = 0
    for b in bits:
        m |= 1 << b
    return m


def _plan(T, topo):
    if "plan" in _CACHE:
        return _CACHE["plan"]
    cores = list(T.cores)
    n = len(cores)
    near = [[d for d in range(n) if d != s and topo.may_write(cores[s], cores[d])] for s in range(n)]
    direct = []
    for s in range(n):
        later = [d for d in near[s] if d > s]
        direct.append(later[0] if later else near[s][0])
    inb = {}
    for s in range(n):
        key = (direct[s], topo.die(cores[s]))
        inb[key] = inb.get(key, 0) + 1
    plan = []
    for s, sc in enumerate(cores):
        rest = [d for d in range(n) if d != s and d != direct[s]]
        far = [d for d in rest if d not in near[s]]
        chipmates = [h for h in range(WORLD)
                     if h != sc and topo.host(h) == topo.host(sc) and topo.chip(h) == topo.chip(sc)]
        owners = [h for h in chipmates if all(topo.may_write(h, cores[d]) for d in far)]
        pools = ([h for h in chipmates if topo.die(h) == topo.die(sc)],
                 [h for h in chipmates if topo.die(h) != topo.die(sc)])
        best = None
        for pick in range(1 << len(rest)):
            groups = ([d for i, d in enumerate(rest) if (pick >> i) & 1],
                      [d for i, d in enumerate(rest) if not (pick >> i) & 1])
            if len(groups[0]) != len(groups[1]):
                continue
            cost, fits = 0, True
            for grp, pool in zip(groups, pools):
                nfar = len([d for d in grp if d in far])
                if nfar > len([h for h in pool if h in owners]) or len(grp) > len(pool):
                    fits = False
                    break
                cost += nfar * nfar
                for d in grp:
                    cost += 2 * inb.get((d, topo.die(pool[0])), 0) + 1
            if fits and (best is None or cost < best[0]):
                best = (cost, groups)
        helpers = []
        for grp, pool in zip(best[1], pools):
            own = [h for h in pool if h in owners]
            plain = [h for h in pool if h not in owners]
            for d in [d for d in grp if d in far]:
                helpers.append((own.pop(0), d))
            for d in [d for d in grp if d not in far]:
                helpers.append(((plain or own).pop(0), d))
        for h, d in helpers:
            key = (d, topo.die(h))
            inb[key] = inb.get(key, 0) + 1
        plan.append((direct[s], helpers))
    _CACHE["plan"] = plan
    return plan


def _transfer(topo, core, src, dsts, mask, remote_sem):
    ids = []
    for d, _ in dsts:
        rid, pid = topo.addr(d, core)
        ids.append(DstId(rid=rid, pnc=pid))
    return RemoteDMATransfer(dst_ids=ids, dma_engine_mask=mask, remote_sem=remote_sem,
                             srcs=[src], dsts=[ap for _, ap in dsts], alu_op=0)


def rank_program(g, core, T, topo):
    cores = list(T.cores)
    n = len(cores)
    plan = _plan(T, topo)
    rank = T.rank_of(core)

    def cslot(s):
        return T.bc[:, s * KC:(s + 1) * KC]

    def xslot(s):
        return T.bx[:, s * TK:(s + 1) * TK]

    def split(s):
        off = _bits(topo.mask(cores[s], cores[plan[s][0]]))
        return off, [b for b in _bits(topo.mask(cores[s], plan[s][1][0][0])) if b not in off]

    if rank is None:
        for s in range(n):
            for h, d in plan[s][1]:
                if h == core:
                    out = topo.mask(core, cores[d])
                    part = len(split(s)[1]) // 2
                    g.wait_ge(T.sem.hx, part)
                    g.remote_dma_fused([_transfer(topo, core, T.px[:, :], [(cores[d], xslot(s))], out, T.sem.xs)],
                                       local_sem=T.sem.sent)
                    g.wait_ge(T.sem.hc, part)
                    g.remote_dma_fused([_transfer(topo, core, T.pc[:, :], [(cores[d], cslot(s))], out,
                                                  T.sem["c%d" % s])], local_sem=T.sem.sent)
                    g.wait_ge(T.sem.sent, 2 * len(_bits(out)))
        return

    nxt, helpers = plan[rank]
    g.sync.dma_start(T.px[:, :], T.x[:, :]).then_inc(T.sem.ldx, 16)
    g.scalar.dma_start(T.pc[:, :], T.c[:, :]).then_inc(T.sem.ldc, 16)
    off, on = split(rank)
    mine = [h for h, _ in helpers if topo.die(h) == topo.die(core)]
    other = [h for h, _ in helpers if topo.die(h) != topo.die(core)]
    g.wait_ge(T.sem.ldx, 16)
    g.remote_dma_fused([_transfer(topo, core, T.px[:, :], [(h, T.px[:, :]) for h in other], _mask(on[0::2]), T.sem.hx),
                        _transfer(topo, core, T.px[:, :], [(h, T.px[:, :]) for h in mine], _mask(on[1::2]), T.sem.hx)],
                       local_sem=T.sem.sent)
    g.wait_ge(T.sem.ldc, 16)
    g.remote_dma_fused([_transfer(topo, core, T.pc[:, :], [(h, T.pc[:, :]) for h in other], _mask(on[0::2]), T.sem.hc),
                        _transfer(topo, core, T.pc[:, :], [(h, T.pc[:, :]) for h in mine], _mask(on[1::2]), T.sem.hc)],
                       local_sem=T.sem.sent)
    g.remote_dma_fused([_transfer(topo, core, T.px[:, :], [(cores[nxt], xslot(rank))], _mask(off), T.sem.xs)],
                       local_sem=T.sem.sent)
    g.remote_dma_fused([_transfer(topo, core, T.pc[:, :], [(cores[nxt], cslot(rank))], _mask(off),
                                  T.sem["c%d" % rank])], local_sem=T.sem.sent)
    g.sem_inc(T.sem.go, 1)
    g.sync.wait_ge(T.sem.go, 1)
    g.sync.dma_start(xslot(rank), T.x[:, :]).then_inc(T.sem.own, 16)
    g.scalar.wait_ge(T.sem.go, 1)
    g.scalar.dma_start(cslot(rank), T.c[:, :]).then_inc(T.sem.own, 16)

    senders = []
    for s in range(n):
        if s == rank:
            continue
        if plan[s][0] == rank:
            senders.append((0, s, cores[s]))
        for h, d in plan[s][1]:
            if d == rank:
                senders.append((1 if topo.same_plane(h, core) else 2, s, h))
    senders.sort()

    te = g.tensor
    te.wait_ge(T.sem.own, 32)
    n_x = 0
    for _, _, h in senders:
        n_x += len(_bits(topo.mask(h, core)))
    te.wait_ge(T.sem.xs, n_x)
    mm = te.matmul(T.acc[:, :], cslot(rank), xslot(0), True, False)
    for i, (_, s, h) in enumerate(senders):
        te.wait_ge(T.sem["c%d" % s], len(_bits(topo.mask(h, core))))
        mm = te.matmul(T.acc[:, :], cslot(s), xslot((rank - s) % n), False, i == len(senders) - 1)
    mm.then_inc(T.sem.mm, 1)
    g.vector.wait_ge(T.sem.mm, 1)
    g.vector.tensor_copy(T.yb[:, :], T.acc[:, :]).then_inc(T.sem.cp, 1)
    g.sync.wait_ge(T.sem.cp, 1)
    g.sync.dma_start(T.y[:, :], T.yb[:, :]).then_inc(T.sem.st, 16)
    g.wait_ge(T.sem.sent, 2 * len(on) + 2 * len(off))
    g.wait_ge(T.sem.st, 16)
